import numpy as np
import ml_dtypes


def mxq(x, axis, fmt="e4m3"):
    dtype, down = {"e4m3": (ml_dtypes.float8_e4m3fn, 7), "e5m2": (ml_dtypes.float8_e5m2, 14)}[fmt]
    v = np.moveaxis(np.asarray(x, np.float32).astype(ml_dtypes.bfloat16).astype(np.float64), axis, -1)
    blocks = v.reshape(v.shape[:-1] + (-1, 32))
    amax = np.abs(blocks).max(-1, keepdims=True)
    byte = np.maximum(np.where(amax > 0, np.frexp(amax)[1] - 1 + 127, 0) - down, 1)
    scale = np.exp2(byte - 127.0)
    codes = (blocks / scale).astype(np.float32).astype(dtype).astype(np.float64)
    return np.moveaxis((codes * scale).reshape(v.shape), -1, axis)


WIDE = False


def mx_kscale(k):
    if not WIDE:
        return np.ones(k)
    levels = np.array([10, -10, 5, -5, 0])
    if k % 512:
        return np.exp2(np.random.permutation(np.resize(levels, k // 32))).repeat(32)
    a = np.empty((k // 512, 16))
    for p in range(k // 512):
        a[p, :8] = np.random.permutation(np.resize(levels, 8))
        for g in range(8):
            far = levels[np.abs(levels - a[p, g]) >= 10]
            a[p, g + 8] = far[np.random.randint(len(far))]
    return np.exp2(a.ravel()).repeat(32)


BF16 = ml_dtypes.bfloat16


def bf(x):
    return np.asarray(x, np.float32).astype(BF16)


def f64(x):
    return np.asarray(x).astype(np.float64)


N1, N2, D, T = 128, 128, 2048, 4


def draw0():
    s, t = mx_kscale(D), mx_kscale(D)
    return {"e1": bf(np.random.standard_normal((N1, D)) * s),
            "e2": bf(np.random.standard_normal((N2, D)) / t),
            "w": bf(np.random.standard_normal((T, D, D)) / np.sqrt(D) / s[:, None] * t),
            "v": bf(np.random.standard_normal((T, D)) * 0.5 * t),
            "b": bf(0.3 + 0.1 * np.random.standard_normal(T)),
            "u": bf(np.random.uniform(0.5, 1.5, T))}


def core(e1, e2, w, v, b, u):
    scale = 1.0 / np.sqrt(e1.shape[1])
    t = mxq(f64(e1), 1, "e4m3") @ mxq(f64(w), 1, "e4m3")
    h = t + f64(v)[:, None, :]
    s = scale * (mxq(h, 2, "e4m3") @ mxq(f64(e2), 1, "e4m3").T)
    z = np.tanh(s + f64(b)[:, None, None])
    return np.sum(f64(u)[:, None, None] * z, axis=0)


def e4m3fn_bytes(y):
    return np.clip(np.asarray(y, np.float64), -448.0, 448.0).astype(np.float32).astype(ml_dtypes.float8_e4m3fn).view(np.uint8)


def e4m3fn_values(b):
    return np.asarray(b, np.uint8).view(ml_dtypes.float8_e4m3fn).astype(np.float64)


def setup_inputs():
    d = draw0()
    x0 = np.asarray(d['e2']).astype(np.float64)
    s = (np.max(np.abs(x0), axis=(0,), keepdims=True) / 448.0).astype(np.float32)
    out = {}
    for k, v in d.items():
        if k == 'e2':
            out['e2_bytes'] = e4m3fn_bytes(x0 / s.astype(np.float64))
            out['e2_scale'] = s
        else:
            out[k] = v
    return out


def reference(e1, e2_bytes, e2_scale, w, v, b, u):
    return core(e1, e4m3fn_values(e2_bytes) * e2_scale.astype(np.float64), w, v, b, u)

@@ -1,0 +1,337 @@
+import math
+from contextlib import ExitStack
+
+import concourse.mybir as mybir
+from concourse.masks import make_identity
+
+F32 = mybir.dt.float32
+BF16 = mybir.dt.bfloat16
+U32 = mybir.dt.uint32
+U8 = mybir.dt.uint8
+F8 = mybir.dt.float8_e4m3fn
+FP8X4 = mybir.dt.float8_e4m3fn_x4
+ALU = mybir.AluOpType
+ACT = mybir.ActivationFunctionType
+
+P = 128
+D = 2048
+T = 4
+CHUNK = 512
+PASSES = D // CHUNK
+FLOPS = 2 * P * D * D * T + 2 * P * P * D * T
+
+GROUP_WIDTHS = ((512, 512, 1024), (1024, 1024), (1024, 1024), (1024, 512, 512))
+VECTOR_SHARE = 0.4375
+PREFETCH = 6
+RAW_BUFS = 8
+
+
+def tile_pairwiseneuraltensorscorer_w_kernel(tc, e1, e2_bytes, e2_scale, w, v, b, u, out):
+    nc = tc.nc
+    with ExitStack() as ctx:
+        const = ctx.enter_context(tc.tile_pool(name="const", bufs=1))
+        raws = ctx.enter_context(tc.tile_pool(name="raws", bufs=RAW_BUFS))
+        work = ctx.enter_context(tc.tile_pool(name="work", bufs=4))
+        psum = ctx.enter_context(tc.psum_pool(name="psum", bufs=1))
+
+        ident32 = const.tile([P, P], F32, name="ident32")
+        make_identity(nc, ident32[:])
+        ident16 = const.tile([P, P], BF16, name="ident16")
+        ctx.enter_context(tc.manual_schedule())
+
+        units = []
+        groups = []
+        for k in range(T):
+            col = 0
+            for width in GROUP_WIDTHS[k]:
+                gi = len(groups)
+                groups.append((k, col, width))
+                for g in range(PASSES):
+                    units.append((gi, k, g, col, width))
+                col += width
+        n_units = len(units)
+        last_group = len(groups) - 1
+
+        raw_t = {}
+        grp_t = {}
+        code_t = {}
+
+        def load(n):
+            gi, k, g, col, width = units[n]
+            raw = raws.tile([P, 4, 1024], BF16, name="raw", tag="raw")
+            view = raw[:].rearrange("p j w -> p (j w)")[:, 0 : 4 * width].rearrange("p (j w) -> p j w", j=4)
+            rows = w[k, g * CHUNK : (g + 1) * CHUNK, col : col + width]
+            nc.sync.dma_start(out=view, in_=rows.rearrange("(p j) w -> p j w", j=4))
+            raw_t[n] = view
+
+        def views(n):
+            gi, k, g, col, width = units[n]
+            if n not in grp_t:
+                grp = work.tile([P, 4096], BF16, name="grp", tag="grp", align_bytes=64)
+                grp_t[n] = grp
+            src = raw_t[n].rearrange("p j (c t q) -> p t c j q", t=4, q=4)
+            dst = grp_t[n][:, 0 : 4 * width].rearrange("p (t c q j) -> p t c j q", t=4, q=4, j=4)
+            n_c = width // 16
+            return src, dst, n_c, int(n_c * VECTOR_SHARE)
+
+        def copy_vector(n):
+            src, dst, n_c, cut = views(n)
+            nc.vector.tensor_copy(out=dst[:, :, 0:cut], in_=src[:, :, 0:cut])
+
+        def copy_scalar(n):
+            src, dst, n_c, cut = views(n)
+            for t in range(4):
+                nc.scalar.copy(out=dst[:, t, cut:n_c], in_=src[:, t, cut:n_c])
+
+        def quantize(n):
+            gi, k, g, col, width = units[n]
+            codes = work.tile([P, 1024], U32, name="codes", tag="codes", bufs=12, align_bytes=64)
+            scales = work.tile([P, 1024], U8, name="scales", tag="scales", bufs=12, align_bytes=64)
+            nc.vector.quantize_mx(
+                out=codes[:, 0:width].bitcast(FP8X4), scales=scales[:, 0:width], in_=grp_t[n][:, 0 : 4 * width]
+            )
+            code_t[n] = (codes, scales)
+
+        b_sb = const.tile([P, T], BF16, name="b_sb")
+        u_sb = const.tile([P, T], BF16, name="u_sb")
+        v_raw = const.tile([P, CHUNK], BF16, name="v_raw")
+        warm = const.tile([P, 1], F32, name="warm")
+        nc.vector.memset(warm[:], 0.0)
+        nc.scalar.activation(out=warm[:], in_=warm[:], func=ACT.Tanh)
+        nc.gpsimd.memset(v_raw[:], 0.0)
+        nc.gpsimd.dma_start(out=v_raw[0:16, :], in_=v.rearrange("k (c e) -> (k c) e", c=4))
+        nc.gpsimd.dma_start(out=b_sb[:], in_=b.partition_broadcast(P))
+        nc.gpsimd.dma_start(out=u_sb[:], in_=u.partition_broadcast(P))
+
+        e1_sb = const.tile([P, D], BF16, name="e1_sb", align_bytes=64)
+        e2_in = const.tile([P, D], U8, name="e2_in", align_bytes=64)
+        e2_sc = const.tile([P, D], F32, name="e2_sc", align_bytes=64)
+        e2_val = const.tile([P, D], BF16, name="e2_val", align_bytes=64)
+        e2_perm = const.tile([P, D], BF16, name="e2_perm", align_bytes=64)
+        e1_grp = const.tile([P, D], BF16, name="e1_grp", align_bytes=64)
+        e2_grp = const.tile([P, D], BF16, name="e2_grp", align_bytes=64)
+        e1_codes = const.tile([P, CHUNK], U32, name="e1_codes", align_bytes=64)
+        e1_scales = const.tile([P, CHUNK], U8, name="e1_scales", align_bytes=64)
+        e2_codes = const.tile([P, CHUNK], U32, name="e2_codes", align_bytes=64)
+        e2_scales = const.tile([P, CHUNK], U8, name="e2_scales", align_bytes=64)
+        v_perm = const.tile([P, 4, P], BF16, name="v_perm")
+        v_cols = const.tile([P, 16, 4], F32, name="v_cols")
+        acc = const.tile([P, P], F32, name="acc")
+
+        def bank(i, shape, dtype):
+            t = psum.tile(shape, dtype, name="bank%d" % i, tag="bank%d" % i)
+            return t
+
+        def prep_v():
+            nc.vector.tensor_copy(out=ident16[:], in_=ident32[:])
+            nc.vector.tensor_copy(
+                out=v_perm[:].rearrange("p t (c q) -> p t c q", q=4),
+                in_=v_raw[:].rearrange("p (c t q) -> p t c q", t=4, q=4),
+            )
+            pv = bank(2, [P, 4, P], BF16)
+            for t in range(4):
+                nc.tensor.transpose(pv[:, t, :], v_perm[:, t, :], ident16[:])
+            nc.scalar.copy(out=v_cols[:], in_=pv[:, :, 0:16].rearrange("p t r -> p r t"))
+
+        def prep_e1():
+            words = e1_sb[:].bitcast(F32)
+            for h in range(2):
+                xt = bank(h, [P, 2, 2, P], F32)
+                for gg in range(2):
+                    for s in range(2):
+                        g = 2 * h + gg
+                        nc.tensor.transpose(xt[:, gg, s, :], words[:, 256 * g + s : 256 * (g + 1) : 2], ident32[:])
+                nc.scalar.copy(
+                    out=e1_grp[:, 1024 * h : 1024 * (h + 1)].bitcast(F32).rearrange("p (g i s) -> p g i s", g=2, s=2),
+                    in_=xt[:].rearrange("p g s i -> p g i s"),
+                )
+
+        def quant_e1():
+            nc.vector.quantize_mx(out=e1_codes[:].bitcast(FP8X4), scales=e1_scales[:], in_=e1_grp[:])
+
+        def value_e2(h):
+            cols = slice(1024 * h, 1024 * (h + 1))
+            nc.vector.tensor_tensor(out=e2_val[:, cols], in0=e2_in[:, cols].bitcast(F8), in1=e2_sc[:, cols], op=ALU.mult)
+
+        def perm_e2():
+            nc.vector.tensor_copy(
+                out=e2_perm[:].rearrange("p (g t c q) -> p g t c q", g=4, t=4, q=4),
+                in_=e2_val[:].rearrange("p (g c t q) -> p g t c q", g=4, t=4, q=4),
+            )
+
+        def turn_e2():
+            for g in range(4):
+                pt = bank(g, [P, 4, P], BF16)
+                for t in range(4):
+                    nc.tensor.transpose(pt[:, t, :], e2_perm[:, g * CHUNK + t * P : g * CHUNK + (t + 1) * P], ident16[:])
+                nc.scalar.copy(
+                    out=e2_grp[:, g * CHUNK : (g + 1) * CHUNK].rearrange("p (i t) -> p i t", t=4),
+                    in_=pt[:].rearrange("p t i -> p i t"),
+                )
+
+        def quant_e2():
+            nc.vector.quantize_mx(out=e2_codes[:].bitcast(FP8X4), scales=e2_scales[:], in_=e2_grp[:])
+
+        hp_t = {}
+        hb_t = {}
+        hq_t = {}
+        sp_t = {}
+        first_unit = {}
+        for n in range(n_units):
+            first_unit.setdefault(units[n][0], n)
+
+        def mm1(out_ap, n, cc, t, start, stop):
+            gi, k, g, col, width = units[n]
+            codes, scales = code_t[n]
+            at = t * (width // 4) + cc * P
+            nc.tensor.matmul_mx(
+                out=out_ap,
+                lhsT=codes[:, at : at + P].bitcast(FP8X4),
+                lhsT_scale=scales[:, at : at + P],
+                rhs=e1_codes[:, g * P : (g + 1) * P].bitcast(FP8X4),
+                rhs_scale=e1_scales[:, g * P : (g + 1) * P],
+                start=start,
+                stop=stop,
+            )
+
+        def stage1(gi, cc):
+            hp = psum.tile([P, 4, P], F32, name="hp", tag="hp", bufs=2)
+            n0 = first_unit[gi]
+            for t in range(4):
+                for g in range(PASSES):
+                    mm1(hp[:, t, :], n0 + g, cc, t, g == 0, g == PASSES - 1)
+            hp_t[(gi, cc)] = hp
+
+        def chunk_of(gi, cc):
+            k, col, width = groups[gi]
+            return k, col // CHUNK + cc
+
+        def h_copy(gi, cc):
+            k, c = chunk_of(gi, cc)
+            hb = work.tile([P, P, 4], BF16, name="hb", tag="hb", bufs=3, align_bytes=64)
+            r = k * 4 + c
+            nc.vector.tensor_tensor(
+                out=hb[:],
+                in0=hp_t[(gi, cc)][:].rearrange("p t i -> p i t"),
+                in1=v_cols[:, r : r + 1, :].to_broadcast([P, P, 4]),
+                op=ALU.add,
+            )
+            hb_t[(gi, cc)] = hb
+
+        def h_quant(gi, cc):
+            hq = work.tile([P, P], U32, name="hq", tag="hq", bufs=8, align_bytes=64)
+            hs = work.tile([P, P], U8, name="hs", tag="hs", bufs=8, align_bytes=64)
+            nc.vector.quantize_mx(
+                out=hq[:].bitcast(FP8X4), scales=hs[:], in_=hb_t[(gi, cc)][:].rearrange("p i t -> p (i t)")
+            )
+            hq_t[(gi, cc)] = (hq, hs)
+
+        def stage2(gi, cc):
+            k, c = chunk_of(gi, cc)
+            if c == 0:
+                sp = psum.tile([P, P], F32, name="sp", tag="sp", bufs=2)
+                sp_t[k] = sp
+            hq, hs = hq_t[(gi, cc)]
+            nc.tensor.matmul_mx(
+                out=sp_t[k][:],
+                lhsT=hq[:].bitcast(FP8X4),
+                lhsT_scale=hs[:],
+                rhs=e2_codes[:, c * P : (c + 1) * P].bitcast(FP8X4),
+                rhs_scale=e2_scales[:, c * P : (c + 1) * P],
+                start=(c == 0),
+                stop=(c == PASSES - 1),
+            )
+
+        def finish(k):
+            z = work.tile([P, P], F32, name="z", tag="z", bufs=2)
+            nc.scalar.activation(
+                out=z[:], in_=sp_t[k][:], func=ACT.Tanh, bias=b_sb[:, k : k + 1], scale=1.0 / math.sqrt(D)
+            )
+            if k == 0:
+                nc.vector.tensor_scalar_mul(out=acc[:], in0=z[:], scalar1=u_sb[:, 0:1])
+            else:
+                nc.vector.scalar_tensor_tensor(
+                    out=acc[:], in0=z[:], scalar=u_sb[:, k : k + 1], in1=acc[:], op0=ALU.mult, op1=ALU.add
+                )
+
+        def extra_load(n):
+            if n == 1:
+                nc.sync.dma_start(out=e1_sb[:], in_=e1)
+            if n == 3:
+                nc.sync.dma_start(out=e2_in[:], in_=e2_bytes)
+                nc.sync.dma_start(out=e2_sc[:], in_=e2_scale.rearrange("o k -> (o k)").partition_broadcast(P))
+
+        for n in range(PREFETCH):
+            load(n)
+            extra_load(n)
+
+        todo_copy = []
+        todo_quant = []
+        todo_mm2 = []
+        todo_finish = []
+        tail = None
+        E2_READY = 9
+        for n in range(n_units + 1):
+            if n + PREFETCH < n_units:
+                load(n + PREFETCH)
+            if n < n_units:
+                copy_scalar(n)
+                copy_vector(n)
+            if n == 1:
+                prep_v()
+            if n == 2:
+                prep_e1()
+            if n == 3:
+                quant_e1()
+            if n == 5:
+                value_e2(0)
+            if n == 6:
+                value_e2(1)
+            if n == 7:
+                perm_e2()
+                turn_e2()
+            if n == 8:
+                quant_e2()
+            done_quants = list(todo_quant)
+            todo_quant.clear()
+            for item in done_quants:
+                h_quant(item[0], item[1])
+                todo_mm2.append(item)
+            if n >= 1:
+                quantize(n - 1)
+                gi = units[n - 1][0]
+                g = units[n - 1][2]
+                if gi == last_group:
+                    if g == 0:
+                        tail = [bank(t, [P, P], F32) for t in range(4)]
+                    for t in range(4):
+                        mm1(tail[t][:], n - 1, 0, t, g == 0, g == PASSES - 1)
+            if todo_copy:
+                item = todo_copy.pop(0)
+                h_copy(item[0], item[1])
+                todo_quant.append(item)
+            if n >= 1 and gi != last_group and g == PASSES - 1:
+                for cc in range(groups[gi][2] // CHUNK):
+                    stage1(gi, cc)
+                    todo_copy.append((gi, cc))
+            if n >= E2_READY:
+                for item in list(todo_mm2):
+                    stage2(item[0], item[1])
+                    k, c = chunk_of(item[0], item[1])
+                    if c == PASSES - 1:
+                        todo_finish.append((n + 2, k))
+                todo_mm2.clear()
+            if todo_finish and todo_finish[0][0] <= n:
+                finish(todo_finish.pop(0)[1])
+
+        r = 15
+        hb = work.tile([P, P, 4], BF16, name="hb", tag="hb", bufs=3, align_bytes=64)
+        for t in range(2):
+            nc.vector.tensor_scalar_add(out=hb[:, :, t], in0=tail[t][:], scalar1=v_cols[:, r, t : t + 1])
+        for t in range(2, 4):
+            nc.scalar.activation(out=hb[:, :, t], in_=tail[t][:], func=ACT.Identity, bias=v_cols[:, r, t : t + 1])
+        hb_t[(last_group, 0)] = hb
+        h_quant(last_group, 0)
+        stage2(last_group, 0)
+        finish(T - 1)
+        nc.sync.dma_start(out=out, in_=acc[:])

@@ -21,8 +21,11 @@ PASSES = D // CHUNK
 FLOPS = 2 * P * D * D * T + 2 * P * P * D * T
 
 GROUP_WIDTHS = ((512, 512, 1024), (1024, 1024), (1024, 1024), (1024, 512, 512))
-VECTOR_SHARE = 0.4375
+CUT_HEAD = 17
+CUT_MID = 28
+CUT_TAIL = 13
 PREFETCH = 6
+ICOLS = 576
 RAW_BUFS = 8
 
 
@@ -54,6 +57,7 @@ def tile_pairwiseneuraltensorscorer_w_kernel(tc, e1, e2_bytes, e2_scale, w, v, b
 
         raw_t = {}
         grp_t = {}
+        pi_t = {}
         code_t = {}
 
         def load(n):
@@ -61,7 +65,12 @@ def tile_pairwiseneuraltensorscorer_w_kernel(tc, e1, e2_bytes, e2_scale, w, v, b
             raw = raws.tile([P, 4, 1024], BF16, name="raw", tag="raw")
             view = raw[:].rearrange("p j w -> p (j w)")[:, 0 : 4 * width].rearrange("p (j w) -> p j w", j=4)
             rows = w[k, g * CHUNK : (g + 1) * CHUNK, col : col + width]
-            nc.sync.dma_start(out=view, in_=rows.rearrange("(p j) w -> p j w", j=4))
+            rows = rows.rearrange("(p j) w -> p j w", j=4)
+            if n == 0:
+                nc.sync.dma_start(out=view[:, :, 0:256], in_=rows[:, :, 0:256])
+                nc.sync.dma_start(out=view[:, :, 256:512], in_=rows[:, :, 256:512])
+            else:
+                nc.sync.dma_start(out=view, in_=rows)
             raw_t[n] = view
 
         def views(n):
@@ -72,7 +81,21 @@ def tile_pairwiseneuraltensorscorer_w_kernel(tc, e1, e2_bytes, e2_scale, w, v, b
             src = raw_t[n].rearrange("p j (c t q) -> p t c j q", t=4, q=4)
             dst = grp_t[n][:, 0 : 4 * width].rearrange("p (t c q j) -> p t c j q", t=4, q=4, j=4)
             n_c = width // 16
-            return src, dst, n_c, int(n_c * VECTOR_SHARE)
+            return src, dst, n_c, CUT_HEAD if n < 8 else CUT_MID if n < 32 else CUT_TAIL
+
+        def spread(n):
+            if n >= n_units or units[n][4] != 1024:
+                return
+            pi = bank(n % 4, [P, ICOLS], BF16)
+            pi_t[n] = pi
+            moving = raw_t[n].rearrange("p j (c t q) -> p t c q j", t=4, q=4)
+            half = ICOLS // 32
+            for s in range(2):
+                c0 = 64 - 2 * half + half * s
+                nc.tensor.matmul(
+                    pi[:, 16 * half * s : 16 * half * (s + 1)].rearrange("p (c q j) -> p c q j", q=4, j=4),
+                    lhsT=ident16[:], rhs=moving[:, 3, c0 : c0 + half], start=True, stop=True,
+                )
 
         def copy_vector(n):
             src, dst, n_c, cut = views(n)
@@ -80,8 +103,14 @@ def tile_pairwiseneuraltensorscorer_w_kernel(tc, e1, e2_bytes, e2_scale, w, v, b
 
         def copy_scalar(n):
             src, dst, n_c, cut = views(n)
-            for t in range(4):
+            ident = n_c == 64
+            for t in range(3 if ident else 4):
                 nc.scalar.copy(out=dst[:, t, cut:n_c], in_=src[:, t, cut:n_c])
+            if ident:
+                at = 3 * 1024 + 16 * (64 - ICOLS // 16)
+                nc.scalar.copy(out=grp_t[n][:, at : at + ICOLS], in_=pi_t[n][:])
+                if 64 - ICOLS // 16 > cut:
+                    nc.scalar.copy(out=dst[:, 3, cut : 64 - ICOLS // 16], in_=src[:, 3, cut : 64 - ICOLS // 16])
 
         def quantize(n):
             gi, k, g, col, width = units[n]
@@ -99,9 +128,6 @@ def tile_pairwiseneuraltensorscorer_w_kernel(tc, e1, e2_bytes, e2_scale, w, v, b
         nc.vector.memset(warm[:], 0.0)
         nc.scalar.activation(out=warm[:], in_=warm[:], func=ACT.Tanh)
         nc.gpsimd.memset(v_raw[:], 0.0)
-        nc.gpsimd.dma_start(out=v_raw[0:16, :], in_=v.rearrange("k (c e) -> (k c) e", c=4))
-        nc.gpsimd.dma_start(out=b_sb[:], in_=b.partition_broadcast(P))
-        nc.gpsimd.dma_start(out=u_sb[:], in_=u.partition_broadcast(P))
 
         e1_sb = const.tile([P, D], BF16, name="e1_sb", align_bytes=64)
         e2_in = const.tile([P, D], U8, name="e2_in", align_bytes=64)
@@ -257,7 +283,10 @@ def tile_pairwiseneuraltensorscorer_w_kernel(tc, e1, e2_bytes, e2_scale, w, v, b
         def extra_load(n):
             if n == 1:
                 nc.sync.dma_start(out=e1_sb[:], in_=e1)
+                nc.sync.dma_start(out=v_raw[0:16, :], in_=v.rearrange("k (c e) -> (k c) e", c=4))
             if n == 3:
+                nc.sync.dma_start(out=b_sb[:], in_=b.partition_broadcast(P))
+                nc.sync.dma_start(out=u_sb[:], in_=u.partition_broadcast(P))
                 nc.sync.dma_start(out=e2_in[:], in_=e2_bytes)
                 nc.sync.dma_start(out=e2_sc[:], in_=e2_scale.rearrange("o k -> (o k)").partition_broadcast(P))
 
@@ -274,23 +303,28 @@ def tile_pairwiseneuraltensorscorer_w_kernel(tc, e1, e2_bytes, e2_scale, w, v, b
         for n in range(n_units + 1):
             if n + PREFETCH < n_units:
                 load(n + PREFETCH)
-            if n < n_units:
-                copy_scalar(n)
-                copy_vector(n)
-            if n == 1:
-                prep_v()
+            if n >= 8:
+                spread(n + 2)
             if n == 2:
                 prep_e1()
             if n == 3:
                 quant_e1()
-            if n == 5:
+            if n == 4:
                 value_e2(0)
-            if n == 6:
                 value_e2(1)
-            if n == 7:
-                perm_e2()
+            if n == 6:
                 turn_e2()
-            if n == 8:
+            if n < n_units:
+                copy_scalar(n)
+                copy_vector(n)
+            if n == 2:
+                prep_v()
+            if n == 5:
+                perm_e2()
+            if n == 6:
+                spread(8)
+            if n == 7:
+                spread(9)
                 quant_e2()
             done_quants = list(todo_quant)
             todo_quant.clear()
@@ -325,11 +359,13 @@ def tile_pairwiseneuraltensorscorer_w_kernel(tc, e1, e2_bytes, e2_scale, w, v, b
                 finish(todo_finish.pop(0)[1])
 
         r = 15
+        ht = const.tile([P, 4, P], BF16, name="ht", align_bytes=64)
         hb = work.tile([P, P, 4], BF16, name="hb", tag="hb", bufs=3, align_bytes=64)
         for t in range(2):
-            nc.vector.tensor_scalar_add(out=hb[:, :, t], in0=tail[t][:], scalar1=v_cols[:, r, t : t + 1])
+            nc.vector.tensor_scalar_add(out=ht[:, t, :], in0=tail[t][:], scalar1=v_cols[:, r, t : t + 1])
         for t in range(2, 4):
-            nc.scalar.activation(out=hb[:, :, t], in_=tail[t][:], func=ACT.Identity, bias=v_cols[:, r, t : t + 1])
+            nc.scalar.activation(out=ht[:, t, :], in_=tail[t][:], func=ACT.Identity, bias=v_cols[:, r, t : t + 1])
+        nc.vector.tensor_copy(out=hb[:], in_=ht[:].rearrange("p t i -> p i t"))
         hb_t[(last_group, 0)] = hb
         h_quant(last_group, 0)
         stage2(last_group, 0)

@@ -20,13 +20,25 @@ CHUNK = 512
 PASSES = D // CHUNK
 FLOPS = 2 * P * D * D * T + 2 * P * P * D * T
 
-GROUP_WIDTHS = ((512, 512, 1024), (1024, 1024), (1024, 1024), (1024, 512, 512))
-CUT_HEAD = 17
-CUT_MID = 28
-CUT_TAIL = 13
-PREFETCH = 6
-ICOLS = 576
-RAW_BUFS = 8
+PLAN = ((0, 0, (1024, 1024)), (1, 0, (1024, 1024)), (2, 0, (1024, 1024)), (3, 0, (1024, 512)), (3, 1536, (512,)))
+HEAD_UNITS = 4
+TAIL_UNITS = 34
+CUT_HEAD = 124
+CUT_MID = 108
+CUT_TAIL = 88
+SPREAD = 36
+FIRST = {
+    (0, 0): ((512, (512,)), (512, (512,)), (512, (512,)), (512, (512,))),
+    (0, 1): ((1024, (1024,)), (1024, (1024,))),
+    (0, 2): ((1024, (1024,)), (1024, (1024,))),
+    (0, 3): ((1024, (1024,)), (1024, (1024,))),
+}
+E1_STEP = 2
+E2_STEP = 6
+SPREAD_FROM = 6
+AHEAD = 2
+PREFETCH = 4
+RAW_BUFS = 4
 
 
 def tile_pairwiseneuraltensorscorer_w_kernel(tc, e1, e2_bytes, e2_scale, w, v, b, u, out):
@@ -38,82 +50,98 @@ def tile_pairwiseneuraltensorscorer_w_kernel(tc, e1, e2_bytes, e2_scale, w, v, b
         psum = ctx.enter_context(tc.psum_pool(name="psum", bufs=1))
 
         ident32 = const.tile([P, P], F32, name="ident32")
-        make_identity(nc, ident32[:])
         ident16 = const.tile([P, P], BF16, name="ident16")
+        v_raw = const.tile([P, CHUNK], BF16, name="v_raw")
+        s_raw = const.tile([P, CHUNK], F32, name="s_raw")
+        make_identity(nc, ident32[:])
         ctx.enter_context(tc.manual_schedule())
+        nc.gpsimd.memset(v_raw[:], 0.0)
+        nc.gpsimd.memset(s_raw[:], 0.0)
 
+        loads = []
         units = []
-        groups = []
-        for k in range(T):
-            col = 0
-            for width in GROUP_WIDTHS[k]:
-                gi = len(groups)
-                groups.append((k, col, width))
-                for g in range(PASSES):
-                    units.append((gi, k, g, col, width))
-                col += width
+        chunk_units = {}
+        for k, col, widths in PLAN:
+            for g in range(PASSES):
+                at = col
+                splits = FIRST.get((k, g), ((sum(widths), widths),))
+                for load_width, unit_widths in splits:
+                    loads.append((k, g, at, load_width))
+                    inner = 0
+                    for width in unit_widths:
+                        n = len(units)
+                        units.append((len(loads) - 1, k, g, at + inner, width, inner, load_width))
+                        for cc in range(width // CHUNK):
+                            chunk_units.setdefault((k, (at + inner) // CHUNK + cc), []).append((n, cc))
+                        inner += width
+                    at += load_width
         n_units = len(units)
-        last_group = len(groups) - 1
+        finishes = {}
+        for key, members in chunk_units.items():
+            finishes.setdefault(members[-1][0], []).append(key)
 
         raw_t = {}
         grp_t = {}
         pi_t = {}
         code_t = {}
 
-        def load(n):
-            gi, k, g, col, width = units[n]
-            raw = raws.tile([P, 4, 1024], BF16, name="raw", tag="raw")
+        def bank(i, shape, dtype):
+            t = psum.tile(shape, dtype, name="bank%d" % i, tag="bank%d" % i)
+            return t
+
+        def load(i):
+            k, g, col, width = loads[i]
+            raw = raws.tile([P, 4, 2048], BF16, name="raw", tag="raw")
             view = raw[:].rearrange("p j w -> p (j w)")[:, 0 : 4 * width].rearrange("p (j w) -> p j w", j=4)
-            rows = w[k, g * CHUNK : (g + 1) * CHUNK, col : col + width]
-            rows = rows.rearrange("(p j) w -> p j w", j=4)
-            if n == 0:
-                nc.sync.dma_start(out=view[:, :, 0:256], in_=rows[:, :, 0:256])
-                nc.sync.dma_start(out=view[:, :, 256:512], in_=rows[:, :, 256:512])
+            rows = w[k, g * CHUNK : (g + 1) * CHUNK, col : col + width].rearrange("(p j) w -> p j w", j=4)
+            if i == 0:
+                for h in range(2):
+                    cols = slice(256 * h, 256 * (h + 1))
+                    nc.sync.dma_start(out=view[:, :, cols], in_=rows[:, :, cols])
             else:
                 nc.sync.dma_start(out=view, in_=rows)
-            raw_t[n] = view
+            raw_t[i] = view
 
-        def views(n):
-            gi, k, g, col, width = units[n]
+        def source(n):
+            li, k, g, col, width, inner, load_width = units[n]
+            return raw_t[li][:, :, inner : inner + width]
+
+        def shares(n):
+            m_all = units[n][4] // 4
+            spread_m = SPREAD if m_all == 256 and n >= SPREAD_FROM else 0
+            cut = CUT_HEAD if n < HEAD_UNITS else CUT_TAIL if n >= TAIL_UNITS else CUT_MID
+            return cut * m_all // 256, m_all - spread_m, m_all
+
+        def grouped(n):
+            width = units[n][4]
             if n not in grp_t:
                 grp = work.tile([P, 4096], BF16, name="grp", tag="grp", align_bytes=64)
                 grp_t[n] = grp
-            src = raw_t[n].rearrange("p j (c t q) -> p t c j q", t=4, q=4)
-            dst = grp_t[n][:, 0 : 4 * width].rearrange("p (t c q j) -> p t c j q", t=4, q=4, j=4)
-            n_c = width // 16
-            return src, dst, n_c, CUT_HEAD if n < 8 else CUT_MID if n < 32 else CUT_TAIL
+            return grp_t[n][:, 0 : 4 * width].rearrange("p (t m j) -> p t m j", t=4, j=4)
+
+        def interleave(n, copy, m0, m1):
+            src = source(n).rearrange("p j (m t) -> p m j t", t=4)
+            copy(out=grouped(n)[:, :, m0:m1].rearrange("p t m j -> p m j t"), in_=src[:, m0:m1])
 
         def spread(n):
             if n >= n_units or units[n][4] != 1024:
                 return
-            pi = bank(n % 4, [P, ICOLS], BF16)
+            pi = bank(n % 4, [P, 4, SPREAD, 4], BF16)
+            src = source(n).rearrange("p j (m t) -> p t m j", t=4)
+            for h in range(2):
+                ts = slice(2 * h, 2 * h + 2)
+                nc.tensor.matmul(pi[:, ts], lhsT=ident16[:], rhs=src[:, ts, 256 - SPREAD : 256], start=True, stop=True)
             pi_t[n] = pi
-            moving = raw_t[n].rearrange("p j (c t q) -> p t c q j", t=4, q=4)
-            half = ICOLS // 32
-            for s in range(2):
-                c0 = 64 - 2 * half + half * s
-                nc.tensor.matmul(
-                    pi[:, 16 * half * s : 16 * half * (s + 1)].rearrange("p (c q j) -> p c q j", q=4, j=4),
-                    lhsT=ident16[:], rhs=moving[:, 3, c0 : c0 + half], start=True, stop=True,
-                )
 
-        def copy_vector(n):
-            src, dst, n_c, cut = views(n)
-            nc.vector.tensor_copy(out=dst[:, :, 0:cut], in_=src[:, :, 0:cut])
-
-        def copy_scalar(n):
-            src, dst, n_c, cut = views(n)
-            ident = n_c == 64
-            for t in range(3 if ident else 4):
-                nc.scalar.copy(out=dst[:, t, cut:n_c], in_=src[:, t, cut:n_c])
-            if ident:
-                at = 3 * 1024 + 16 * (64 - ICOLS // 16)
-                nc.scalar.copy(out=grp_t[n][:, at : at + ICOLS], in_=pi_t[n][:])
-                if 64 - ICOLS // 16 > cut:
-                    nc.scalar.copy(out=dst[:, 3, cut : 64 - ICOLS // 16], in_=src[:, 3, cut : 64 - ICOLS // 16])
+        def copies(n):
+            cut, m1, m_all = shares(n)
+            interleave(n, nc.scalar.copy, cut, m1)
+            if m1 < m_all:
+                nc.scalar.copy(out=grouped(n)[:, :, m1:m_all], in_=pi_t[n][:])
+            interleave(n, nc.vector.tensor_copy, 0, cut)
 
         def quantize(n):
-            gi, k, g, col, width = units[n]
+            width = units[n][4]
             codes = work.tile([P, 1024], U32, name="codes", tag="codes", bufs=12, align_bytes=64)
             scales = work.tile([P, 1024], U8, name="scales", tag="scales", bufs=12, align_bytes=64)
             nc.vector.quantize_mx(
@@ -123,91 +151,81 @@ def tile_pairwiseneuraltensorscorer_w_kernel(tc, e1, e2_bytes, e2_scale, w, v, b
 
         b_sb = const.tile([P, T], BF16, name="b_sb")
         u_sb = const.tile([P, T], BF16, name="u_sb")
-        v_raw = const.tile([P, CHUNK], BF16, name="v_raw")
         warm = const.tile([P, 1], F32, name="warm")
         nc.vector.memset(warm[:], 0.0)
         nc.scalar.activation(out=warm[:], in_=warm[:], func=ACT.Tanh)
-        nc.gpsimd.memset(v_raw[:], 0.0)
 
         e1_sb = const.tile([P, D], BF16, name="e1_sb", align_bytes=64)
         e2_in = const.tile([P, D], U8, name="e2_in", align_bytes=64)
-        e2_sc = const.tile([P, D], F32, name="e2_sc", align_bytes=64)
         e2_val = const.tile([P, D], BF16, name="e2_val", align_bytes=64)
-        e2_perm = const.tile([P, D], BF16, name="e2_perm", align_bytes=64)
         e1_grp = const.tile([P, D], BF16, name="e1_grp", align_bytes=64)
         e2_grp = const.tile([P, D], BF16, name="e2_grp", align_bytes=64)
         e1_codes = const.tile([P, CHUNK], U32, name="e1_codes", align_bytes=64)
         e1_scales = const.tile([P, CHUNK], U8, name="e1_scales", align_bytes=64)
         e2_codes = const.tile([P, CHUNK], U32, name="e2_codes", align_bytes=64)
         e2_scales = const.tile([P, CHUNK], U8, name="e2_scales", align_bytes=64)
-        v_perm = const.tile([P, 4, P], BF16, name="v_perm")
         v_cols = const.tile([P, 16, 4], F32, name="v_cols")
+        s_cols = const.tile([P, 4, 2, 2], F32, name="s_cols")
         acc = const.tile([P, P], F32, name="acc")
 
-        def bank(i, shape, dtype):
-            t = psum.tile(shape, dtype, name="bank%d" % i, tag="bank%d" % i)
-            return t
+        def turn_words(tile_ap, h, xt):
+            words = tile_ap.bitcast(F32)
+            for gg in range(2):
+                for s in range(2):
+                    g = 2 * h + gg
+                    nc.tensor.transpose(xt[:, gg, s, :], words[:, 256 * g + s : 256 * (g + 1) : 2], ident32[:])
+            return xt
 
         def prep_v():
-            nc.vector.tensor_copy(out=ident16[:], in_=ident32[:])
-            nc.vector.tensor_copy(
-                out=v_perm[:].rearrange("p t (c q) -> p t c q", q=4),
-                in_=v_raw[:].rearrange("p (c t q) -> p t c q", t=4, q=4),
-            )
             pv = bank(2, [P, 4, P], BF16)
             for t in range(4):
-                nc.tensor.transpose(pv[:, t, :], v_perm[:, t, :], ident16[:])
+                nc.tensor.transpose(pv[:, t, :], v_raw[:, t:CHUNK:4], ident16[:])
             nc.scalar.copy(out=v_cols[:], in_=pv[:, :, 0:16].rearrange("p t r -> p r t"))
+            ps = bank(3, [P, 4, P], F32)
+            for t in range(4):
+                nc.tensor.transpose(ps[:, t, :], s_raw[:, t:CHUNK:4], ident32[:])
+            nc.scalar.copy(out=s_cols[:].rearrange("p g a c -> p g (a c)"), in_=ps[:, :, 0:4].rearrange("p t r -> p r t"))
 
         def prep_e1():
-            words = e1_sb[:].bitcast(F32)
             for h in range(2):
-                xt = bank(h, [P, 2, 2, P], F32)
-                for gg in range(2):
-                    for s in range(2):
-                        g = 2 * h + gg
-                        nc.tensor.transpose(xt[:, gg, s, :], words[:, 256 * g + s : 256 * (g + 1) : 2], ident32[:])
+                xt = turn_words(e1_sb[:], h, bank(h, [P, 2, 2, P], F32))
                 nc.scalar.copy(
-                    out=e1_grp[:, 1024 * h : 1024 * (h + 1)].bitcast(F32).rearrange("p (g i s) -> p g i s", g=2, s=2),
-                    in_=xt[:].rearrange("p g s i -> p g i s"),
+                    out=e1_grp[:, 1024 * h : 1024 * (h + 1)].bitcast(F32).rearrange("p (g i a) -> p g i a", g=2, a=2),
+                    in_=xt[:].rearrange("p g a i -> p g i a"),
                 )
 
         def quant_e1():
             nc.vector.quantize_mx(out=e1_codes[:].bitcast(FP8X4), scales=e1_scales[:], in_=e1_grp[:])
 
-        def value_e2(h):
-            cols = slice(1024 * h, 1024 * (h + 1))
-            nc.vector.tensor_tensor(out=e2_val[:, cols], in0=e2_in[:, cols].bitcast(F8), in1=e2_sc[:, cols], op=ALU.mult)
-
-        def perm_e2():
-            nc.vector.tensor_copy(
-                out=e2_perm[:].rearrange("p (g t c q) -> p g t c q", g=4, t=4, q=4),
-                in_=e2_val[:].rearrange("p (g c t q) -> p g t c q", g=4, t=4, q=4),
-            )
+        def widen_e2():
+            nc.vector.tensor_copy(out=e2_val[:], in_=e2_in[:].bitcast(F8))
 
         def turn_e2():
+            for h in range(2):
+                xt = psum.tile([P, 2, 2, P], F32, name="xt2", tag="sp", bufs=2)
+                e2_turned.append(turn_words(e2_val[:], h, xt))
+
+        def scale_e2():
             for g in range(4):
-                pt = bank(g, [P, 4, P], BF16)
-                for t in range(4):
-                    nc.tensor.transpose(pt[:, t, :], e2_perm[:, g * CHUNK + t * P : g * CHUNK + (t + 1) * P], ident16[:])
-                nc.scalar.copy(
-                    out=e2_grp[:, g * CHUNK : (g + 1) * CHUNK].rearrange("p (i t) -> p i t", t=4),
-                    in_=pt[:].rearrange("p t i -> p i t"),
+                nc.vector.tensor_tensor(
+                    out=e2_grp[:, g * CHUNK : (g + 1) * CHUNK].rearrange("p (i a c) -> p i a c", a=2, c=2),
+                    in0=e2_turned[g // 2][:, g % 2].bitcast(BF16).rearrange("p a (i c) -> p i a c", c=2),
+                    in1=s_cols[:, g : g + 1].to_broadcast([P, P, 2, 2]),
+                    op=ALU.mult,
                 )
 
         def quant_e2():
             nc.vector.quantize_mx(out=e2_codes[:].bitcast(FP8X4), scales=e2_scales[:], in_=e2_grp[:])
 
+        e2_turned = []
         hp_t = {}
         hb_t = {}
         hq_t = {}
         sp_t = {}
-        first_unit = {}
-        for n in range(n_units):
-            first_unit.setdefault(units[n][0], n)
 
         def mm1(out_ap, n, cc, t, start, stop):
-            gi, k, g, col, width = units[n]
+            g = units[n][2]
+            width = units[n][4]
             codes, scales = code_t[n]
             at = t * (width // 4) + cc * P
             nc.tensor.matmul_mx(
@@ -220,44 +238,40 @@ def tile_pairwiseneuraltensorscorer_w_kernel(tc, e1, e2_bytes, e2_scale, w, v, b
                 stop=stop,
             )
 
-        def stage1(gi, cc):
+        def stage1(key):
             hp = psum.tile([P, 4, P], F32, name="hp", tag="hp", bufs=2)
-            n0 = first_unit[gi]
             for t in range(4):
-                for g in range(PASSES):
-                    mm1(hp[:, t, :], n0 + g, cc, t, g == 0, g == PASSES - 1)
-            hp_t[(gi, cc)] = hp
+                for n, cc in chunk_units[key]:
+                    g = units[n][2]
+                    mm1(hp[:, t, :], n, cc, t, g == 0, g == PASSES - 1)
+            hp_t[key] = hp
 
-        def chunk_of(gi, cc):
-            k, col, width = groups[gi]
-            return k, col // CHUNK + cc
-
-        def h_copy(gi, cc):
-            k, c = chunk_of(gi, cc)
+        def h_copy(key):
+            k, c = key
             hb = work.tile([P, P, 4], BF16, name="hb", tag="hb", bufs=3, align_bytes=64)
             r = k * 4 + c
             nc.vector.tensor_tensor(
                 out=hb[:],
-                in0=hp_t[(gi, cc)][:].rearrange("p t i -> p i t"),
+                in0=hp_t[key][:].rearrange("p t i -> p i t"),
                 in1=v_cols[:, r : r + 1, :].to_broadcast([P, P, 4]),
                 op=ALU.add,
             )
-            hb_t[(gi, cc)] = hb
+            hb_t[key] = hb
 
-        def h_quant(gi, cc):
+        def h_quant(key):
             hq = work.tile([P, P], U32, name="hq", tag="hq", bufs=8, align_bytes=64)
             hs = work.tile([P, P], U8, name="hs", tag="hs", bufs=8, align_bytes=64)
             nc.vector.quantize_mx(
-                out=hq[:].bitcast(FP8X4), scales=hs[:], in_=hb_t[(gi, cc)][:].rearrange("p i t -> p (i t)")
+                out=hq[:].bitcast(FP8X4), scales=hs[:], in_=hb_t[key][:].rearrange("p i t -> p (i t)")
             )
-            hq_t[(gi, cc)] = (hq, hs)
+            hq_t[key] = (hq, hs)
 
-        def stage2(gi, cc):
-            k, c = chunk_of(gi, cc)
+        def stage2(key):
+            k, c = key
             if c == 0:
                 sp = psum.tile([P, P], F32, name="sp", tag="sp", bufs=2)
                 sp_t[k] = sp
-            hq, hs = hq_t[(gi, cc)]
+            hq, hs = hq_t[key]
             nc.tensor.matmul_mx(
                 out=sp_t[k][:],
                 lhsT=hq[:].bitcast(FP8X4),
@@ -284,90 +298,91 @@ def tile_pairwiseneuraltensorscorer_w_kernel(tc, e1, e2_bytes, e2_scale, w, v, b
             if n == 1:
                 nc.sync.dma_start(out=e1_sb[:], in_=e1)
                 nc.sync.dma_start(out=v_raw[0:16, :], in_=v.rearrange("k (c e) -> (k c) e", c=4))
-            if n == 3:
+                nc.sync.dma_start(out=s_raw[0:4, :], in_=e2_scale.rearrange("o (g e) -> (o g) e", g=4))
+            if n == 5:
+                nc.sync.dma_start(out=e2_in[:], in_=e2_bytes)
                 nc.sync.dma_start(out=b_sb[:], in_=b.partition_broadcast(P))
                 nc.sync.dma_start(out=u_sb[:], in_=u.partition_broadcast(P))
-                nc.sync.dma_start(out=e2_in[:], in_=e2_bytes)
-                nc.sync.dma_start(out=e2_sc[:], in_=e2_scale.rearrange("o k -> (o k)").partition_broadcast(P))
 
-        for n in range(PREFETCH):
-            load(n)
-            extra_load(n)
+        LAST = (T - 1, PASSES - 1)
+        n_loads = len(loads)
+        loaded = 0
+        while loaded < PREFETCH:
+            load(loaded)
+            extra_load(loaded)
+            loaded += 1
 
+        todo_mm1 = []
         todo_copy = []
         todo_quant = []
         todo_mm2 = []
         todo_finish = []
         tail = None
-        E2_READY = 9
+        spread_next = SPREAD_FROM
+        nc.vector.tensor_copy(out=ident16[:], in_=ident32[:])
         for n in range(n_units + 1):
-            if n + PREFETCH < n_units:
-                load(n + PREFETCH)
-            if n >= 8:
-                spread(n + 2)
-            if n == 2:
+            while loaded < n_loads and n < n_units and loaded < units[n][0] + PREFETCH:
+                load(loaded)
+                extra_load(loaded)
+                loaded += 1
+            if n == E1_STEP:
                 prep_e1()
-            if n == 3:
-                quant_e1()
-            if n == 4:
-                value_e2(0)
-                value_e2(1)
-            if n == 6:
-                turn_e2()
-            if n < n_units:
-                copy_scalar(n)
-                copy_vector(n)
-            if n == 2:
                 prep_v()
-            if n == 5:
-                perm_e2()
-            if n == 6:
-                spread(8)
-            if n == 7:
-                spread(9)
+            if n == E1_STEP + 1:
+                quant_e1()
+            if n == E2_STEP:
+                widen_e2()
+                turn_e2()
+            if n == E2_STEP + 1:
+                scale_e2()
+            if n < n_units:
+                copies(n)
+            if n == E2_STEP + 2:
                 quant_e2()
             done_quants = list(todo_quant)
             todo_quant.clear()
-            for item in done_quants:
-                h_quant(item[0], item[1])
-                todo_mm2.append(item)
+            for key in done_quants:
+                h_quant(key)
+                todo_mm2.append(key)
             if n >= 1:
                 quantize(n - 1)
-                gi = units[n - 1][0]
-                g = units[n - 1][2]
-                if gi == last_group:
+                k, g, col = units[n - 1][1:4]
+                if (k, col // CHUNK) == LAST:
                     if g == 0:
                         tail = [bank(t, [P, P], F32) for t in range(4)]
                     for t in range(4):
                         mm1(tail[t][:], n - 1, 0, t, g == 0, g == PASSES - 1)
-            if todo_copy:
-                item = todo_copy.pop(0)
-                h_copy(item[0], item[1])
-                todo_quant.append(item)
-            if n >= 1 and gi != last_group and g == PASSES - 1:
-                for cc in range(groups[gi][2] // CHUNK):
-                    stage1(gi, cc)
-                    todo_copy.append((gi, cc))
-            if n >= E2_READY:
-                for item in list(todo_mm2):
-                    stage2(item[0], item[1])
-                    k, c = chunk_of(item[0], item[1])
-                    if c == PASSES - 1:
-                        todo_finish.append((n + 2, k))
+            if todo_copy and todo_copy[0][0] <= n:
+                key = todo_copy.pop(0)[1]
+                h_copy(key)
+                todo_quant.append(key)
+            if n >= 1:
+                todo_mm1.extend(key for key in finishes.get(n - 1, []) if key != LAST)
+            if todo_mm1 and len(todo_copy) < 2:
+                key = todo_mm1.pop(0)
+                stage1(key)
+                todo_copy.append((n + (1 if n < TAIL_UNITS else 2), key))
+            if n > E2_STEP + 2:
+                for key in list(todo_mm2):
+                    stage2(key)
+                    if key[1] == PASSES - 1:
+                        todo_finish.append((n + 2, key[0]))
                 todo_mm2.clear()
+            while spread_next <= n + AHEAD:
+                spread(spread_next)
+                spread_next += 1
             if todo_finish and todo_finish[0][0] <= n:
                 finish(todo_finish.pop(0)[1])
 
-        r = 15
         ht = const.tile([P, 4, P], BF16, name="ht", align_bytes=64)
         hb = work.tile([P, P, 4], BF16, name="hb", tag="hb", bufs=3, align_bytes=64)
         for t in range(2):
-            nc.vector.tensor_scalar_add(out=ht[:, t, :], in0=tail[t][:], scalar1=v_cols[:, r, t : t + 1])
+            nc.vector.tensor_scalar_add(out=ht[:, t, :], in0=tail[t][:], scalar1=v_cols[:, 15, t : t + 1])
         for t in range(2, 4):
-            nc.scalar.activation(out=ht[:, t, :], in_=tail[t][:], func=ACT.Identity, bias=v_cols[:, r, t : t + 1])
+            nc.scalar.activation(out=ht[:, t, :], in_=tail[t][:], func=ACT.Identity, bias=v_cols[:, 15, t : t + 1])
         nc.vector.tensor_copy(out=hb[:], in_=ht[:].rearrange("p t i -> p i t"))
-        hb_t[(last_group, 0)] = hb
-        h_quant(last_group, 0)
-        stage2(last_group, 0)
+        hb_t[LAST] = hb
+        h_quant(LAST)
+        stage2(LAST)
         finish(T - 1)
         nc.sync.dma_start(out=out, in_=acc[:])

@@ -21,21 +21,20 @@ PASSES = D // CHUNK
 FLOPS = 2 * P * D * D * T + 2 * P * P * D * T
 
 PLAN = ((0, 0, (1024, 1024)), (1, 0, (1024, 1024)), (2, 0, (1024, 1024)), (3, 0, (1024, 512)), (3, 1536, (512,)))
-HEAD_UNITS = 4
-TAIL_UNITS = 34
-CUT_HEAD = 124
-CUT_MID = 108
-CUT_TAIL = 88
+HEAD_UNITS = 3
+TAIL_UNITS = 32
+CUT_HEAD = 128
+CUT_MID = 96
+CUT_TAIL = 80
 SPREAD = 36
 FIRST = {
-    (0, 0): ((512, (512,)), (512, (512,)), (512, (512,)), (512, (512,))),
+    (0, 0): ((512, (512,)), (512, (512,)), (1024, (1024,))),
     (0, 1): ((1024, (1024,)), (1024, (1024,))),
     (0, 2): ((1024, (1024,)), (1024, (1024,))),
-    (0, 3): ((1024, (1024,)), (1024, (1024,))),
 }
 E1_STEP = 2
-E2_STEP = 6
-SPREAD_FROM = 6
+E2_STEP = 2
+SPREAD_FROM = 5
 AHEAD = 2
 PREFETCH = 4
 RAW_BUFS = 4
@@ -138,7 +137,9 @@ def tile_pairwiseneuraltensorscorer_w_kernel(tc, e1, e2_bytes, e2_scale, w, v, b
             interleave(n, nc.scalar.copy, cut, m1)
             if m1 < m_all:
                 nc.scalar.copy(out=grouped(n)[:, :, m1:m_all], in_=pi_t[n][:])
-            interleave(n, nc.vector.tensor_copy, 0, cut)
+            src = source(n).rearrange("p j (a m t) -> p a j t m", m=2, t=4)
+            dst = grouped(n).rearrange("p t (a m) j -> p a j t m", m=2)
+            nc.vector.tensor_copy(out=dst[:, 0 : cut // 2], in_=src[:, 0 : cut // 2])
 
         def quantize(n):
             width = units[n][4]
@@ -248,10 +249,14 @@ def tile_pairwiseneuraltensorscorer_w_kernel(tc, e1, e2_bytes, e2_scale, w, v, b
 
         def h_copy(key):
             k, c = key
-            hb = work.tile([P, P, 4], BF16, name="hb", tag="hb", bufs=3, align_bytes=64)
             r = k * 4 + c
+            if (k, c) not in SINGLE and c % 2 == 1:
+                hb = hb_t[(k, c - 1)]
+            else:
+                hb = work.tile([P, 2, P, 4], BF16, name="hb", tag="hb", bufs=3, align_bytes=64)
+            half = 0 if (k, c) in SINGLE else c % 2
             nc.vector.tensor_tensor(
-                out=hb[:],
+                out=hb[:, half],
                 in0=hp_t[key][:].rearrange("p t i -> p i t"),
                 in1=v_cols[:, r : r + 1, :].to_broadcast([P, P, 4]),
                 op=ALU.add,
@@ -259,12 +264,17 @@ def tile_pairwiseneuraltensorscorer_w_kernel(tc, e1, e2_bytes, e2_scale, w, v, b
             hb_t[key] = hb
 
         def h_quant(key):
-            hq = work.tile([P, P], U32, name="hq", tag="hq", bufs=8, align_bytes=64)
-            hs = work.tile([P, P], U8, name="hs", tag="hs", bufs=8, align_bytes=64)
+            n_h = 1 if key in SINGLE else 2
+            hq = work.tile([P, 2 * P], U32, name="hq", tag="hq", bufs=6, align_bytes=64)
+            hs = work.tile([P, 2 * P], U8, name="hs", tag="hs", bufs=6, align_bytes=64)
             nc.vector.quantize_mx(
-                out=hq[:].bitcast(FP8X4), scales=hs[:], in_=hb_t[key][:].rearrange("p i t -> p (i t)")
+                out=hq[:, 0 : n_h * P].bitcast(FP8X4),
+                scales=hs[:, 0 : n_h * P],
+                in_=hb_t[key][:, 0:n_h].rearrange("p h i t -> p (h i t)"),
             )
-            hq_t[key] = (hq, hs)
+            for h in range(n_h):
+                cols = slice(h * P, (h + 1) * P)
+                hq_t[(key[0], key[1] - (n_h - 1) + h)] = (hq[:, cols], hs[:, cols])
 
         def stage2(key):
             k, c = key
@@ -274,8 +284,8 @@ def tile_pairwiseneuraltensorscorer_w_kernel(tc, e1, e2_bytes, e2_scale, w, v, b
             hq, hs = hq_t[key]
             nc.tensor.matmul_mx(
                 out=sp_t[k][:],
-                lhsT=hq[:].bitcast(FP8X4),
-                lhsT_scale=hs[:],
+                lhsT=hq.bitcast(FP8X4),
+                lhsT_scale=hs,
                 rhs=e2_codes[:, c * P : (c + 1) * P].bitcast(FP8X4),
                 rhs_scale=e2_scales[:, c * P : (c + 1) * P],
                 start=(c == 0),
@@ -299,12 +309,14 @@ def tile_pairwiseneuraltensorscorer_w_kernel(tc, e1, e2_bytes, e2_scale, w, v, b
                 nc.sync.dma_start(out=e1_sb[:], in_=e1)
                 nc.sync.dma_start(out=v_raw[0:16, :], in_=v.rearrange("k (c e) -> (k c) e", c=4))
                 nc.sync.dma_start(out=s_raw[0:4, :], in_=e2_scale.rearrange("o (g e) -> (o g) e", g=4))
-            if n == 5:
+            if n == 1:
                 nc.sync.dma_start(out=e2_in[:], in_=e2_bytes)
+            if n == 4:
                 nc.sync.dma_start(out=b_sb[:], in_=b.partition_broadcast(P))
                 nc.sync.dma_start(out=u_sb[:], in_=u.partition_broadcast(P))
 
         LAST = (T - 1, PASSES - 1)
+        SINGLE = ((T - 1, 2), LAST)
         n_loads = len(loads)
         loaded = 0
         while loaded < PREFETCH:
@@ -343,6 +355,8 @@ def tile_pairwiseneuraltensorscorer_w_kernel(tc, e1, e2_bytes, e2_scale, w, v, b
             todo_quant.clear()
             for key in done_quants:
                 h_quant(key)
+                if key not in SINGLE:
+                    todo_mm2.append((key[0], key[1] - 1))
                 todo_mm2.append(key)
             if n >= 1:
                 quantize(n - 1)
@@ -355,7 +369,8 @@ def tile_pairwiseneuraltensorscorer_w_kernel(tc, e1, e2_bytes, e2_scale, w, v, b
             if todo_copy and todo_copy[0][0] <= n:
                 key = todo_copy.pop(0)[1]
                 h_copy(key)
-                todo_quant.append(key)
+                if key in SINGLE or key[1] % 2 == 1:
+                    todo_quant.append(key)
             if n >= 1:
                 todo_mm1.extend(key for key in finishes.get(n - 1, []) if key != LAST)
             if todo_mm1 and len(todo_copy) < 2:
@@ -375,12 +390,12 @@ def tile_pairwiseneuraltensorscorer_w_kernel(tc, e1, e2_bytes, e2_scale, w, v, b
                 finish(todo_finish.pop(0)[1])
 
         ht = const.tile([P, 4, P], BF16, name="ht", align_bytes=64)
-        hb = work.tile([P, P, 4], BF16, name="hb", tag="hb", bufs=3, align_bytes=64)
+        hb = work.tile([P, 2, P, 4], BF16, name="hb", tag="hb", bufs=3, align_bytes=64)
         for t in range(2):
             nc.vector.tensor_scalar_add(out=ht[:, t, :], in0=tail[t][:], scalar1=v_cols[:, 15, t : t + 1])
         for t in range(2, 4):
             nc.scalar.activation(out=ht[:, t, :], in_=tail[t][:], func=ACT.Identity, bias=v_cols[:, 15, t : t + 1])
-        nc.vector.tensor_copy(out=hb[:], in_=ht[:].rearrange("p t i -> p i t"))
+        nc.vector.tensor_copy(out=hb[:, 0], in_=ht[:].rearrange("p t i -> p i t"))
         hb_t[LAST] = hb
         h_quant(LAST)
         stage2(LAST)

import math
from contextlib import ExitStack

import concourse.mybir as mybir
from concourse.masks import make_identity

F32 = mybir.dt.float32
BF16 = mybir.dt.bfloat16
U32 = mybir.dt.uint32
U8 = mybir.dt.uint8
F8 = mybir.dt.float8_e4m3fn
FP8X4 = mybir.dt.float8_e4m3fn_x4
ALU = mybir.AluOpType
ACT = mybir.ActivationFunctionType

P = 128
D = 2048
T = 4
CHUNK = 512
PASSES = D // CHUNK
FLOPS = 2 * P * D * D * T + 2 * P * P * D * T

PLAN = ((0, 0, (1024, 1024)), (1, 0, (1024, 1024)), (2, 0, (1024, 1024)), (3, 0, (1024, 512)), (3, 1536, (512,)))
HEAD_UNITS = 3
TAIL_UNITS = 32
CUT_HEAD = 128
CUT_MID = 96
CUT_TAIL = 80
SPREAD = 36
FIRST = {
    (0, 0): ((512, (512,)), (512, (512,)), (1024, (1024,))),
    (0, 1): ((1024, (1024,)), (1024, (1024,))),
    (0, 2): ((1024, (1024,)), (1024, (1024,))),
}
E1_STEP = 2
E2_STEP = 2
SPREAD_FROM = 5
AHEAD = 2
PREFETCH = 4
RAW_BUFS = 4


def tile_pairwiseneuraltensorscorer_w_kernel(tc, e1, e2_bytes, e2_scale, w, v, b, u, out):
    nc = tc.nc
    with ExitStack() as ctx:
        const = ctx.enter_context(tc.tile_pool(name="const", bufs=1))
        raws = ctx.enter_context(tc.tile_pool(name="raws", bufs=RAW_BUFS))
        work = ctx.enter_context(tc.tile_pool(name="work", bufs=4))
        psum = ctx.enter_context(tc.psum_pool(name="psum", bufs=1))

        ident32 = const.tile([P, P], F32, name="ident32")
        ident16 = const.tile([P, P], BF16, name="ident16")
        v_raw = const.tile([P, CHUNK], BF16, name="v_raw")
        s_raw = const.tile([P, CHUNK], F32, name="s_raw")
        make_identity(nc, ident32[:])
        ctx.enter_context(tc.manual_schedule())
        nc.gpsimd.memset(v_raw[:], 0.0)
        nc.gpsimd.memset(s_raw[:], 0.0)

        loads = []
        units = []
        chunk_units = {}
        for k, col, widths in PLAN:
            for g in range(PASSES):
                at = col
                splits = FIRST.get((k, g), ((sum(widths), widths),))
                for load_width, unit_widths in splits:
                    loads.append((k, g, at, load_width))
                    inner = 0
                    for width in unit_widths:
                        n = len(units)
                        units.append((len(loads) - 1, k, g, at + inner, width, inner, load_width))
                        for cc in range(width // CHUNK):
                            chunk_units.setdefault((k, (at + inner) // CHUNK + cc), []).append((n, cc))
                        inner += width
                    at += load_width
        n_units = len(units)
        finishes = {}
        for key, members in chunk_units.items():
            finishes.setdefault(members[-1][0], []).append(key)

        raw_t = {}
        grp_t = {}
        pi_t = {}
        code_t = {}

        def bank(i, shape, dtype):
            t = psum.tile(shape, dtype, name="bank%d" % i, tag="bank%d" % i)
            return t

        def load(i):
            k, g, col, width = loads[i]
            raw = raws.tile([P, 4, 2048], BF16, name="raw", tag="raw")
            view = raw[:].rearrange("p j w -> p (j w)")[:, 0 : 4 * width].rearrange("p (j w) -> p j w", j=4)
            rows = w[k, g * CHUNK : (g + 1) * CHUNK, col : col + width].rearrange("(p j) w -> p j w", j=4)
            if i == 0:
                for h in range(2):
                    cols = slice(256 * h, 256 * (h + 1))
                    nc.sync.dma_start(out=view[:, :, cols], in_=rows[:, :, cols])
            else:
                nc.sync.dma_start(out=view, in_=rows)
            raw_t[i] = view

        def source(n):
            li, k, g, col, width, inner, load_width = units[n]
            return raw_t[li][:, :, inner : inner + width]

        def shares(n):
            m_all = units[n][4] // 4
            spread_m = SPREAD if m_all == 256 and n >= SPREAD_FROM else 0
            cut = CUT_HEAD if n < HEAD_UNITS else CUT_TAIL if n >= TAIL_UNITS else CUT_MID
            return cut * m_all // 256, m_all - spread_m, m_all

        def grouped(n):
            width = units[n][4]
            if n not in grp_t:
                grp = work.tile([P, 4096], BF16, name="grp", tag="grp", align_bytes=64)
                grp_t[n] = grp
            return grp_t[n][:, 0 : 4 * width].rearrange("p (t m j) -> p t m j", t=4, j=4)

        def interleave(n, copy, m0, m1):
            src = source(n).rearrange("p j (m t) -> p m j t", t=4)
            copy(out=grouped(n)[:, :, m0:m1].rearrange("p t m j -> p m j t"), in_=src[:, m0:m1])

        def spread(n):
            if n >= n_units or units[n][4] != 1024:
                return
            pi = bank(n % 4, [P, 4, SPREAD, 4], BF16)
            src = source(n).rearrange("p j (m t) -> p t m j", t=4)
            for h in range(2):
                ts = slice(2 * h, 2 * h + 2)
                nc.tensor.matmul(pi[:, ts], lhsT=ident16[:], rhs=src[:, ts, 256 - SPREAD : 256], start=True, stop=True)
            pi_t[n] = pi

        def copies(n):
            cut, m1, m_all = shares(n)
            interleave(n, nc.scalar.copy, cut, m1)
            if m1 < m_all:
                nc.scalar.copy(out=grouped(n)[:, :, m1:m_all], in_=pi_t[n][:])
            src = source(n).rearrange("p j (a m t) -> p a j t m", m=2, t=4)
            dst = grouped(n).rearrange("p t (a m) j -> p a j t m", m=2)
            nc.vector.tensor_copy(out=dst[:, 0 : cut // 2], in_=src[:, 0 : cut // 2])

        def quantize(n):
            width = units[n][4]
            codes = work.tile([P, 1024], U32, name="codes", tag="codes", bufs=12, align_bytes=64)
            scales = work.tile([P, 1024], U8, name="scales", tag="scales", bufs=12, align_bytes=64)
            nc.vector.quantize_mx(
                out=codes[:, 0:width].bitcast(FP8X4), scales=scales[:, 0:width], in_=grp_t[n][:, 0 : 4 * width]
            )
            code_t[n] = (codes, scales)

        b_sb = const.tile([P, T], BF16, name="b_sb")
        u_sb = const.tile([P, T], BF16, name="u_sb")
        warm = const.tile([P, 1], F32, name="warm")
        nc.vector.memset(warm[:], 0.0)
        nc.scalar.activation(out=warm[:], in_=warm[:], func=ACT.Tanh)

        e1_sb = const.tile([P, D], BF16, name="e1_sb", align_bytes=64)
        e2_in = const.tile([P, D], U8, name="e2_in", align_bytes=64)
        e2_val = const.tile([P, D], BF16, name="e2_val", align_bytes=64)
        e1_grp = const.tile([P, D], BF16, name="e1_grp", align_bytes=64)
        e2_grp = const.tile([P, D], BF16, name="e2_grp", align_bytes=64)
        e1_codes = const.tile([P, CHUNK], U32, name="e1_codes", align_bytes=64)
        e1_scales = const.tile([P, CHUNK], U8, name="e1_scales", align_bytes=64)
        e2_codes = const.tile([P, CHUNK], U32, name="e2_codes", align_bytes=64)
        e2_scales = const.tile([P, CHUNK], U8, name="e2_scales", align_bytes=64)
        v_cols = const.tile([P, 16, 4], F32, name="v_cols")
        s_cols = const.tile([P, 4, 2, 2], F32, name="s_cols")
        acc = const.tile([P, P], F32, name="acc")

        def turn_words(tile_ap, h, xt):
            words = tile_ap.bitcast(F32)
            for gg in range(2):
                for s in range(2):
                    g = 2 * h + gg
                    nc.tensor.transpose(xt[:, gg, s, :], words[:, 256 * g + s : 256 * (g + 1) : 2], ident32[:])
            return xt

        def prep_v():
            pv = bank(2, [P, 4, P], BF16)
            for t in range(4):
                nc.tensor.transpose(pv[:, t, :], v_raw[:, t:CHUNK:4], ident16[:])
            nc.scalar.copy(out=v_cols[:], in_=pv[:, :, 0:16].rearrange("p t r -> p r t"))
            ps = bank(3, [P, 4, P], F32)
            for t in range(4):
                nc.tensor.transpose(ps[:, t, :], s_raw[:, t:CHUNK:4], ident32[:])
            nc.scalar.copy(out=s_cols[:].rearrange("p g a c -> p g (a c)"), in_=ps[:, :, 0:4].rearrange("p t r -> p r t"))

        def prep_e1():
            for h in range(2):
                xt = turn_words(e1_sb[:], h, bank(h, [P, 2, 2, P], F32))
                nc.scalar.copy(
                    out=e1_grp[:, 1024 * h : 1024 * (h + 1)].bitcast(F32).rearrange("p (g i a) -> p g i a", g=2, a=2),
                    in_=xt[:].rearrange("p g a i -> p g i a"),
                )

        def quant_e1():
            nc.vector.quantize_mx(out=e1_codes[:].bitcast(FP8X4), scales=e1_scales[:], in_=e1_grp[:])

        def widen_e2():
            nc.vector.tensor_copy(out=e2_val[:], in_=e2_in[:].bitcast(F8))

        def turn_e2():
            for h in range(2):
                xt = psum.tile([P, 2, 2, P], F32, name="xt2", tag="sp", bufs=2)
                e2_turned.append(turn_words(e2_val[:], h, xt))

        def scale_e2():
            for g in range(4):
                nc.vector.tensor_tensor(
                    out=e2_grp[:, g * CHUNK : (g + 1) * CHUNK].rearrange("p (i a c) -> p i a c", a=2, c=2),
                    in0=e2_turned[g // 2][:, g % 2].bitcast(BF16).rearrange("p a (i c) -> p i a c", c=2),
                    in1=s_cols[:, g : g + 1].to_broadcast([P, P, 2, 2]),
                    op=ALU.mult,
                )

        def quant_e2():
            nc.vector.quantize_mx(out=e2_codes[:].bitcast(FP8X4), scales=e2_scales[:], in_=e2_grp[:])

        e2_turned = []
        hp_t = {}
        hb_t = {}
        hq_t = {}
        sp_t = {}

        def mm1(out_ap, n, cc, t, start, stop):
            g = units[n][2]
            width = units[n][4]
            codes, scales = code_t[n]
            at = t * (width // 4) + cc * P
            nc.tensor.matmul_mx(
                out=out_ap,
                lhsT=codes[:, at : at + P].bitcast(FP8X4),
                lhsT_scale=scales[:, at : at + P],
                rhs=e1_codes[:, g * P : (g + 1) * P].bitcast(FP8X4),
                rhs_scale=e1_scales[:, g * P : (g + 1) * P],
                start=start,
                stop=stop,
            )

        def stage1(key):
            hp = psum.tile([P, 4, P], F32, name="hp", tag="hp", bufs=2)
            for t in range(4):
                for n, cc in chunk_units[key]:
                    g = units[n][2]
                    mm1(hp[:, t, :], n, cc, t, g == 0, g == PASSES - 1)
            hp_t[key] = hp

        def h_copy(key):
            k, c = key
            r = k * 4 + c
            if (k, c) not in SINGLE and c % 2 == 1:
                hb = hb_t[(k, c - 1)]
            else:
                hb = work.tile([P, 2, P, 4], BF16, name="hb", tag="hb", bufs=3, align_bytes=64)
            half = 0 if (k, c) in SINGLE else c % 2
            nc.vector.tensor_tensor(
                out=hb[:, half],
                in0=hp_t[key][:].rearrange("p t i -> p i t"),
                in1=v_cols[:, r : r + 1, :].to_broadcast([P, P, 4]),
                op=ALU.add,
            )
            hb_t[key] = hb

        def h_quant(key):
            n_h = 1 if key in SINGLE else 2
            hq = work.tile([P, 2 * P], U32, name="hq", tag="hq", bufs=6, align_bytes=64)
            hs = work.tile([P, 2 * P], U8, name="hs", tag="hs", bufs=6, align_bytes=64)
            nc.vector.quantize_mx(
                out=hq[:, 0 : n_h * P].bitcast(FP8X4),
                scales=hs[:, 0 : n_h * P],
                in_=hb_t[key][:, 0:n_h].rearrange("p h i t -> p (h i t)"),
            )
            for h in range(n_h):
                cols = slice(h * P, (h + 1) * P)
                hq_t[(key[0], key[1] - (n_h - 1) + h)] = (hq[:, cols], hs[:, cols])

        def stage2(key):
            k, c = key
            if c == 0:
                sp = psum.tile([P, P], F32, name="sp", tag="sp", bufs=2)
                sp_t[k] = sp
            hq, hs = hq_t[key]
            nc.tensor.matmul_mx(
                out=sp_t[k][:],
                lhsT=hq.bitcast(FP8X4),
                lhsT_scale=hs,
                rhs=e2_codes[:, c * P : (c + 1) * P].bitcast(FP8X4),
                rhs_scale=e2_scales[:, c * P : (c + 1) * P],
                start=(c == 0),
                stop=(c == PASSES - 1),
            )

        def finish(k):
            z = work.tile([P, P], F32, name="z", tag="z", bufs=2)
            nc.scalar.activation(
                out=z[:], in_=sp_t[k][:], func=ACT.Tanh, bias=b_sb[:, k : k + 1], scale=1.0 / math.sqrt(D)
            )
            if k == 0:
                nc.vector.tensor_scalar_mul(out=acc[:], in0=z[:], scalar1=u_sb[:, 0:1])
            else:
                nc.vector.scalar_tensor_tensor(
                    out=acc[:], in0=z[:], scalar=u_sb[:, k : k + 1], in1=acc[:], op0=ALU.mult, op1=ALU.add
                )

        def extra_load(n):
            if n == 1:
                nc.sync.dma_start(out=e1_sb[:], in_=e1)
                nc.sync.dma_start(out=v_raw[0:16, :], in_=v.rearrange("k (c e) -> (k c) e", c=4))
                nc.sync.dma_start(out=s_raw[0:4, :], in_=e2_scale.rearrange("o (g e) -> (o g) e", g=4))
            if n == 1:
                nc.sync.dma_start(out=e2_in[:], in_=e2_bytes)
            if n == 4:
                nc.sync.dma_start(out=b_sb[:], in_=b.partition_broadcast(P))
                nc.sync.dma_start(out=u_sb[:], in_=u.partition_broadcast(P))

        LAST = (T - 1, PASSES - 1)
        SINGLE = ((T - 1, 2), LAST)
        n_loads = len(loads)
        loaded = 0
        while loaded < PREFETCH:
            load(loaded)
            extra_load(loaded)
            loaded += 1

        todo_mm1 = []
        todo_copy = []
        todo_quant = []
        todo_mm2 = []
        todo_finish = []
        tail = None
        spread_next = SPREAD_FROM
        nc.vector.tensor_copy(out=ident16[:], in_=ident32[:])
        for n in range(n_units + 1):
            while loaded < n_loads and n < n_units and loaded < units[n][0] + PREFETCH:
                load(loaded)
                extra_load(loaded)
                loaded += 1
            if n == E1_STEP:
                prep_e1()
                prep_v()
            if n == E1_STEP + 1:
                quant_e1()
            if n == E2_STEP:
                widen_e2()
                turn_e2()
            if n == E2_STEP + 1:
                scale_e2()
            if n < n_units:
                copies(n)
            if n == E2_STEP + 2:
                quant_e2()
            done_quants = list(todo_quant)
            todo_quant.clear()
            for key in done_quants:
                h_quant(key)
                if key not in SINGLE:
                    todo_mm2.append((key[0], key[1] - 1))
                todo_mm2.append(key)
            if n >= 1:
                quantize(n - 1)
                k, g, col = units[n - 1][1:4]
                if (k, col // CHUNK) == LAST:
                    if g == 0:
                        tail = [bank(t, [P, P], F32) for t in range(4)]
                    for t in range(4):
                        mm1(tail[t][:], n - 1, 0, t, g == 0, g == PASSES - 1)
            if todo_copy and todo_copy[0][0] <= n:
                key = todo_copy.pop(0)[1]
                h_copy(key)
                if key in SINGLE or key[1] % 2 == 1:
                    todo_quant.append(key)
            if n >= 1:
                todo_mm1.extend(key for key in finishes.get(n - 1, []) if key != LAST)
            if todo_mm1 and len(todo_copy) < 2:
                key = todo_mm1.pop(0)
                stage1(key)
                todo_copy.append((n + (1 if n < TAIL_UNITS else 2), key))
            if n > E2_STEP + 2:
                for key in list(todo_mm2):
                    stage2(key)
                    if key[1] == PASSES - 1:
                        todo_finish.append((n + 2, key[0]))
                todo_mm2.clear()
            while spread_next <= n + AHEAD:
                spread(spread_next)
                spread_next += 1
            if todo_finish and todo_finish[0][0] <= n:
                finish(todo_finish.pop(0)[1])

        ht = const.tile([P, 4, P], BF16, name="ht", align_bytes=64)
        hb = work.tile([P, 2, P, 4], BF16, name="hb", tag="hb", bufs=3, align_bytes=64)
        for t in range(2):
            nc.vector.tensor_scalar_add(out=ht[:, t, :], in0=tail[t][:], scalar1=v_cols[:, 15, t : t + 1])
        for t in range(2, 4):
            nc.scalar.activation(out=ht[:, t, :], in_=tail[t][:], func=ACT.Identity, bias=v_cols[:, 15, t : t + 1])
        nc.vector.tensor_copy(out=hb[:, 0], in_=ht[:].rearrange("p t i -> p i t"))
        hb_t[LAST] = hb
        h_quant(LAST)
        stage2(LAST)
        finish(T - 1)
        nc.sync.dma_start(out=out, in_=acc[:])
